import numpy as np, ml_dtypes
CORES = [40,64,80,88,96,104,120,144]
N = 8
import mx_ref
BF = ml_dtypes.bfloat16
def gcols(t, e):
    v = np.concatenate([t.reshape(8, 16, -1, 4), np.zeros((8, 16, 1, 4), BF)], axis=2)
    return np.ascontiguousarray(np.stack([v[g][:, e[g]] for g in range(8)])).reshape(128, -1)
def tile(rs):
    return np.stack(rs, axis=2).reshape(128, -1).astype(BF)
def cut(t, i, w=512):
    return t[:, w * i:w * i + w]
def gentries(a):
    return np.ascontiguousarray(a.reshape(8, 16, -1).transpose(0, 2, 1)).reshape(8, -1)
def gtable(e):
    e = np.asarray(e); return np.ascontiguousarray(e.reshape(8, -1, 16).transpose(0, 2, 1)).reshape(128, -1).astype(np.int32)
def pick(q, e):
    c = np.concatenate([q[0].reshape(128, -1, 4), np.zeros((128, 1, 4), np.uint8)], axis=1); s = np.concatenate([q[1], np.ones((16, 1), np.uint8)], axis=1)
    return (np.ascontiguousarray(c[:, e].reshape(128, -1)), np.ascontiguousarray(s[:, e]))
def join(*qs):
    return (np.concatenate([q[0] for q in qs], axis=1), np.concatenate([q[1] for q in qs], axis=1))
def put(q, e, v):
    c, s = q[0].reshape(128, -1, 4).copy(), q[1].copy(); c[:, e] = v[0].reshape(128, -1, 4); s[:, e] = v[1]
    return (c.reshape(128, -1), s)
def pk(c, s):
    return (np.ascontiguousarray(c), mx_ref.live(s))
def emit(q):
    return q[0], q[1]
def packed(v, rng):
    q = [mx_ref.quantize(np.ascontiguousarray(v[r])) for r in range(N)]
    return np.stack([a for a, b in q]), np.stack([mx_ref.plane(b, rng) for a, b in q])
def values_of_codes():
    e, c = np.zeros((128, 128, 4), np.float32), np.zeros((128, 2, 4), np.uint8)
    e[np.arange(128), np.arange(128), 0] = 1
    c[:127, :, 0] = np.arange(256).reshape(2, 128).T[:127]
    return mx_ref.matmul(mx_ref.quantize(e.reshape(128, 512).astype(BF)), (c.reshape(128, 8), np.full((16, 2), 127, np.uint8))).T.reshape(-1).astype(np.float64)
CODE_VALUE, SCALE_VALUE = values_of_codes(), 2.0 ** (np.arange(256) - 127.0)
def decode(q):
    return (CODE_VALUE[q[0]].reshape(16, 8, -1, 4) * SCALE_VALUE[q[1]][:, None, :, None] + 0.0).reshape(128, -1).astype(np.float32)
def f(rng, *shape):
    return mx_ref.flush((rng.standard_normal(shape, dtype=np.float32) * np.exp2(rng.integers(-2, 3, shape[:-1] + (1,)))).astype(BF))
def wide(rng, *shape, cols=0):
    v = rng.standard_normal(shape, dtype=np.float32) * np.exp2(rng.integers(-12, 13, shape)).astype(np.float32)
    if cols: v *= np.repeat(np.exp2(rng.integers(-cols, cols + 1, shape[:-2] + (1, shape[-1] // 4))) * (rng.random(shape[:-2] + (1, shape[-1] // 4)) > 0.0625), 4, axis=-1).astype(np.float32)
    return mx_ref.flush(v.astype(BF))
C, B, R = 224, 96, 3
def order(p):
    return np.argsort(-(p[::16] + np.float32(0.0)), axis=1, kind="stable")
def big(v):
    v = v.astype(np.float32)
    v[np.abs(v) < np.float32(2.0 ** -16)] = 0
    return v.astype(BF)
def numbers_of(rng):
    return {"x": big(f(rng, N, 128, 16 * C)), "u": np.array(f(rng, N, 128, 512)), "v": np.array(f(rng, N, 128, 512))}
def weights(rng, kept=[]):
    w = np.array(f(rng, N, 128, 2048)).reshape(N, 8, 16, 4, 8, 16, 4)
    for i in kept:
        w[:, :, i] = 0
        w[:, :, :, :, :, i] = 0
        for g in range(8):
            for k in range(4): w[:, g, i, k, g, i, k] = 32
    c, p = packed(w.reshape(N, 128, 2048), rng)
    return {"wc": c, "ws": p}
def paths(rng):
    a = np.zeros((N, 8, C), int)
    for r in range(N):
        for g in range(8):
            a[r, g, ::2] = rng.permutation(C // 2) * 2 + 1
            a[r, g, 1::2] = rng.permutation(C // 2) * 2
    return [a, rng.integers(0, B, (N, 8, C)), rng.integers(0, 4, (N, 8, C)), rng.integers(0, 4, (N, 8, C))]
def stored(p):
    return {k: np.stack([gtable(e[r]) for r in range(N)]) for k, e in zip(("la", "lb", "da", "db"), p)}
def plant(rng, p, z):
    x = np.zeros((N, 8, 16, 4, C, 4), np.float32)
    at = np.zeros((N, 8, C), int)
    for r in range(N):
        for g in range(8):
            a = p[0][r, g]
            at[r, g, a] = p[2][r, g]
            x[r, g][:, :, a] = z[r, g][:, None]
            x[r, g][:, :, :B][:, np.arange(4)[:, None] != at[r, g, :B]] = 0
    for r in range(N): p[3][r] = (np.take_along_axis(at[r - 1], p[1][r], axis=1) + rng.integers(1, 4, (8, C))) % 4
    return x.reshape(N, 128, 16 * C).astype(BF)
def signs(rng):
    return np.stack([rng.permutation(8) % 2 * 2.0 - 1.0 for r in range(N)])
def setup_inputs(rng):
    return {**numbers_of(rng), **weights(rng), **stored(paths(rng))}
def setup_inputs_ties(rng):
    d = numbers_of(rng)
    e = rng.permutation(N)
    x = d["x"].reshape(N, 8, 16, 4, C, 4)
    for r in range(N):
        k = np.zeros((4, C), int) if r == e[0] else rng.integers(0, 3, (4, C))
        a = x[r][:, :8, 0, :3].copy()
        a[:, :, 2] = 0
        x[r][:, :8] = a[:, :, k]
    x[e[1]] = 0
    u = d["u"].reshape(N, 8, 16, 8, 16, 4)
    k = u.copy()
    u[:, :, :, :, :2] = 0
    for g in range(8): u[:, g, :8, g, :2] = k[:, g, :8, g, :2]
    return {"x": x.reshape(N, 128, 16 * C), "u": u.reshape(N, 128, 512), "v": d["v"], **weights(rng, range(8)), **stored(paths(rng))}
def setup_inputs_near(rng):
    d = numbers_of(rng)
    p = paths(rng)
    z = np.zeros((N, 8, 16, C, 4), np.float32)
    u = d["u"].reshape(N, 128, 128, 4)
    u[:, :, ::16] = 0
    u[:, :, 1::16] = 0
    o, c = rng.permutation(N) % 4, signs(rng)
    upper = np.arange(C) // (C // 2)
    for r in range(N):
        i = (np.arange(C) + rng.integers(0, C, (8, 1))) % C
        if o[r] == 3: i = i % (C // 2) * 2 + upper
        s = (i + 1) // 2
        size = 1.0 if o[r] < 2 else 2.0 ** -4
        m = ((s[:, :, None] >> np.arange(8)) & 1) * np.exp2(np.arange(8) - 22.0) * size
        if o[r] < 2:
            z[r, :, 0, :, 0] = 2 * c[r][:, None]
            for g in rng.permutation(8)[:4]: z[r, g, 0, rng.integers(C), 0] *= np.float32(2.0 ** 29)
        if o[r] == 3: z[r, :, 0, :, 0] = (8 + upper) * 2.0 ** -29
        z[r, :, 1, :, 0] = rng.integers(-1, 2, (8, C)) * (2.0 if o[r] < 2 else 2.0 ** -26)
        z[r, :, 8] = m[:, :, :4]
        z[r, :, 9] = m[:, :, 4:]
        z[r, :, 10:] = rng.integers(4, 8, (8, 6, C, 4)) * 2.0 ** -19 * size
        k = 1.0 if o[r] == 0 else 2.0 ** -30
        for h in range(0, 128, 16):
            u[r, h, h, 0] = k
            u[r, h + 8:h + 10, h] = k
            u[r, h + 1, h + 1, 0] = k
    x = plant(rng, p, z)
    return {"x": x, "u": u.reshape(N, 128, 512), "v": d["v"], **weights(rng, range(16)), **stored(p)}
def setup_inputs_lags(rng):
    d = numbers_of(rng)
    p = paths(rng)
    p[2] = rng.integers(1, 3, (N, 8, C))
    x = d["x"].astype(np.float32).reshape(N, 8, 16, 4, C, 4)
    u = d["u"].reshape(N, 128, 128, 4)
    u[:, :, 1::16] = 0
    kind = rng.permutation(8)
    ends = [(3, 3), (0, 0), (9, 9), (9, 9), (9, 0), (9, 3), (3, 9), (9, 9)]
    for g in range(8):
        k = kind[g]
        x[:, g, 0, :, :, 0] = rng.integers(4, 8, (N, 4, C)) * 0.25 * [1, -1, 1, -1, 1, -1, 1, 0][k]
        u[:, 16 * g, 16 * g + 1, 0] = 1
        for i in range(2):
            if ends[k][i] < 9: p[2][:, g, i::2] = ends[k][i]
        if k == 2: p[0][:, g] = np.arange(C) ^ 1
        if k == 3: p[0][:, g] = (np.arange(C) + 1) % C
        if k == 4: p[1][:, g], p[3][:, g] = rng.integers(B), 0
        if k == 5: p[3][:, g] = 3
    return {"x": x.reshape(N, 128, 16 * C).astype(BF), "u": u.reshape(N, 128, 512), "v": d["v"], **weights(rng, [0]), **stored(p)}
def setup_inputs_huge(rng):
    d = numbers_of(rng)
    p = paths(rng)
    c = np.stack([rng.permutation(C) % 2 * 2.0 - 1.0 for r in range(N)])
    c[rng.permutation(N) < N // 2] = -1
    z = 2.0 ** 30 * (0.8 + 0.2 * rng.random((N, 8, 16, C, 4))) * c[:, None, None, :, None]
    x = plant(rng, p, z.astype(np.float32))
    u = d["u"].reshape(N, 128, 8, 16, 4)
    a = 2.0 ** 30 * (1 - 0.1 * rng.random((N, 128, 8, 2, 4))) * np.stack([signs(rng), signs(rng)], axis=2)[:, None, :, :, None]
    u[:, :, :, :2] = a.astype(np.float32).astype(BF)
    return {"x": x, "u": u.reshape(N, 128, 512), "v": d["v"], **weights(rng, range(16)), **stored(p)}
def setup_inputs_spread(rng):
    d = setup_inputs(rng)
    d["x"] = big(wide(rng, N, 128, 16 * C, cols=6))
    return d
def check_inputs(d):
    b = []
    for k in ("x", "u", "v"):
        a = np.abs(d[k].astype(np.float32))
        if not (np.isfinite(a).all() and ((a == 0) | (a >= 2.0 ** -30) & (a <= 2.0 ** 30)).all()): b.append("a value of " + k)
    none, least, most = [emit(mx_ref.quantize(np.full((128, 16), k, np.float32).astype(BF)))[1][0, 0] for k in (0.0, 2.0 ** -30, 2.0 ** 30)]
    for r in range(N):
        if ((d["wc"][r] == 0x7F) | (d["wc"][r] == 0xFF)).any(): b.append("wc: a code that is no number")
        s = mx_ref.live(d["ws"][r])
        if ((s != none) & ((s < least) | (s > most))).any(): b.append("ws: a scale out of range")
        a = gentries(d["la"][r])
        if (np.sort(a, axis=1) != np.arange(C)).any(): b.append("la: no permutation")
        if ((a + np.arange(C)) % 2 != 1).any(): b.append("la: a number of the same parity")
        for k, n in (("lb", B), ("da", 4), ("db", 4)):
            if ((d[k][r] < 0) | (d[k][r] >= n)).any(): b.append(k + " out of range")
    return b
def reference(x, u, v, wc, ws, la, lb, da, db):
    qu = [mx_ref.quantize(u[r]) for r in range(N)]
    lay = [pk(wc[r], ws[r]) for r in range(N)]
    ring = [x[r] for r in range(N)]
    came = decode(join(*[mx_ref.quantize(np.ascontiguousarray(x[r].reshape(128, 4, C, 4)[:, :, :B]).reshape(128, -1)) for r in range(N)])).astype(BF)
    edge = [cut(came, (r - 1) % N, 16 * B) for r in range(N)]
    lag = np.zeros((N, 8, C), np.int64)
    last = [None] * N
    for t in range(R):
        sent = []
        for r in range(N):
            a = gentries(la[r])
            delay = gentries(da[r]) + lag[r] - np.take_along_axis(lag[r], a, axis=1)
            own = gcols(ring[r], C * delay + a)
            far = gcols(edge[r], B * gentries(db[r]) + gentries(lb[r]))
            q = mx_ref.quantize(((own.astype(np.float32) + far.astype(np.float32)) * np.float32(0.5)).astype(BF))
            s = mx_ref.matmul(qu[r], q)
            h = tile([mx_ref.matmul(pick(lay[r], np.arange(128 * b, 128 * b + 128)), q) * np.float32(0.03125) for b in range(4)])
            last[r] = h
            ring[r] = np.concatenate([h, ring[r][:, :12 * C]], axis=1)
            sent.append(mx_ref.quantize(gcols(h, order(s)[:, :B])))
            step = ((s[1::16] > 0).astype(np.int64) - (s[1::16] < 0)) * (np.arange(C) % 2 == t % 2)
            one = delay + step
            two = np.take_along_axis(delay, np.argsort(a, axis=1), axis=1) - step
            lag[r] += np.where((one >= 0) & (one <= 3) & (two >= 0) & (two <= 3), step, 0)
        if t < R - 1:
            came = decode(join(*sent)).astype(BF)
            edge = [np.concatenate([cut(came, (r - 1) % N, 4 * B), edge[r][:, :12 * B]], axis=1) for r in range(N)]
    y, ol = np.zeros((N, 128, C), np.float32), np.zeros((N, 8, C), np.float32)
    oc, osc = np.zeros((N, 128, 4 * C), np.uint8), np.zeros((N, 16, C), np.uint8)
    for r in range(N):
        q = mx_ref.quantize(last[r])
        y[r] = mx_ref.matmul(mx_ref.quantize(v[r]), q)
        ol[r] = lag[r]
        oc[r], osc[r] = emit(q)
    return {"y": y, "ol": ol, "oc": oc, "osc": osc}

from concourse.bass import DstId, RemoteDMATransfer
from concourse.mybir import dt, AluOpType, ActivationFunctionType

C, B, R = 224, 96, 3
K = C // 16
W4 = 4 * C
FW = 4 * B + 2 * C
NV = 9
NA = K - NV
BIG = 1.0e29
CODE, PLANE = "float8_e4m3fn_x4", "uint8"


def _sb(n, d):
    return ("sbuf", [128, n], d)


SCRATCH = {
    "ps": ("psum", [128, 4096], "float32"),
    "xb": _sb(16 * B, "bfloat16"), "qb": _sb(4 * B, CODE), "sb": _sb(4 * B, PLANE),
    "ring": _sb(6 * W4, "bfloat16"), "hl": _sb(W4, "bfloat16"),
    "far": _sb(4 * FW, "bfloat16"), "own": _sb(W4, "bfloat16"), "z": _sb(W4, "bfloat16"),
    "ut": _sb(512, "bfloat16"), "qu": _sb(128, CODE), "su": _sb(128, PLANE),
    "u0c": _sb(128, CODE), "u0s": _sb(128, PLANE), "u1c": _sb(128, CODE), "u1s": _sb(128, PLANE),
    "vt": _sb(512, "bfloat16"), "qv": _sb(128, CODE), "sv": _sb(128, PLANE),
    "wq": _sb(512, CODE), "wp": _sb(512, PLANE),
    "ones": _sb(128, "bfloat16"), "ident": _sb(128, "bfloat16"), "et": _sb(2048, "bfloat16"),
    "qe": _sb(512, CODE), "se": _sb(512, PLANE),
    "lst": _sb(64, "int32"), "nbi": _sb(C, "int32"), "nbj": _sb(C, "int32"), "upi": _sb(8, "int32"), "up16": _sb(16, "uint16"),
    "nb": _sb(C, "float32"), "kk": _sb(C, "float32"), "mm": _sb(C, "bfloat16"), "m3": _sb(3 * NA, "float32"),
    "ew": _sb(5 * B + C, "float32"), "io2": _sb(2 * C, "float32"), "dw": _sb(8, "float32"),
    "a16": _sb(K, "uint16"), "f16": _sb(K, "uint16"), "c16": _sb(K, "uint16"), "fo16": _sb(K, "uint16"),
    "fz16": _sb(K, "uint16"), "o16": _sb(4 * K, "uint16"),
    "a4": _sb(K, "float32"), "t1": _sb(K, "float32"), "t2": _sb(K, "float32"), "t3": _sb(K, "float32"), "t4": _sb(K, "float32"),
    "crow": _sb(C, "float32"), "lr": _sb(C, "float32"), "ls": _sb(C, "float32"), "fr": _sb(C, "float32"), "fs": _sb(C, "float32"),
    "nd0": _sb(C, "float32"), "nd1": _sb(C, "float32"), "nd2": _sb(C, "float32"), "dr": _sb(C, "float32"),
    "lo": _sb(C // 2, "float32"), "hm": _sb(C // 2, "float32"), "hi": _sb(C // 2, "float32"),
    "sg": _sb(C // 2, "float32"), "p1": _sb(C // 2, "float32"), "p2": _sb(C // 2, "float32"),
    "tau0": _sb(C, "float32"), "tau1": _sb(C, "float32"), "olb": _sb(C, "float32"),
    "sr": _sb(C, "float32"), "st": _sb(C, "float32"), "eq": _sb(C, "bfloat16"), "nq": _sb(C, "bfloat16"),
    "cmp": _sb(NV * C, "bfloat16"), "sc": _sb(NV * (C // 2), "bfloat16"),
    "sgn": _sb(NA * C, "bfloat16"), "junk": _sb(NA * C, "bfloat16"), "acc": _sb(3 * NA, "float32"), "asum": _sb(3 * NA, "float32"),
    "ysb": _sb(C, "float32"),
    "hc0": _sb(4 * B, CODE), "hs0": _sb(4 * B, PLANE), "lc0": _sb(4 * B, CODE), "lp0": _sb(4 * B, PLANE),
}
for _t in range(R):
    SCRATCH["tq%d" % _t] = _sb(C, CODE)
    SCRATCH["tp%d" % _t] = _sb(C, PLANE)
    SCRATCH["hq%d" % _t] = _sb(C, CODE)
    SCRATCH["hp%d" % _t] = _sb(C, PLANE)
for _t in range(1, R):
    SCRATCH["hc%d" % _t] = _sb(C, CODE)
    SCRATCH["hs%d" % _t] = _sb(C, PLANE)
    SCRATCH["lc%d" % _t] = _sb(C, CODE)
    SCRATCH["lp%d" % _t] = _sb(C, PLANE)
    SCRATCH["ro%d" % _t] = _sb(K, "uint16")
    SCRATCH["rh%d" % _t] = _sb(K, "uint16")
    SCRATCH["ri%d" % _t] = _sb(K, "uint16")

SEMAPHORES = ["ve", "ac", "pe", "po", "dxa", "dxb", "dl", "du", "dx", "dwt", "dv", "dout", "left0", "left",
              "m0", "m1", "m2", "k1", "k2", "h0", "h1", "h2", "h3"]


def _mask(engines):
    return sum(1 << e for e in engines)


def routes(T, topo, rank):
    src, dst = T.cores[rank], T.cores[(rank + 1) % len(T.cores)]
    calls = []
    if topo.may_write(src, dst):
        e = topo.engines(src, dst)

        def one(msg, s, d):
            calls.append((msg, [(None, e, s, None, d, None)]))
        one("m0a", ("qb", 0, 2 * B), ("lc0", 0, 2 * B))
        one("m0b", ("qb", 2 * B, 4 * B), ("lc0", 2 * B, 4 * B))
        one("m0b", ("sb", 0, 4 * B), ("lp0", 0, 4 * B))
        for t in (1, 2):
            one("m%d" % t, ("hq%d" % (t - 1), 0, C), ("lc%d" % t, 0, C))
            one("m%d" % t, ("hp%d" % (t - 1), 0, C), ("lp%d" % t, 0, C))
            one("k%d" % t, ("ro%d" % t, 0, K), ("ri%d" % t, 0, K))
        return calls
    rel = [c for c in topo.cores_of(src) if T.rank_of(c) is None and topo.may_write(c, dst)]
    rel.sort(key=lambda c: (topo.die(c) != topo.die(src), c))
    e = topo.engines(src, rel[0])
    n = len(e)

    def piece(k, eng, s, h, d, a, b, sem):
        return (rel[k], eng, (s, a, b), (h, a, b), (d, a, b), sem)
    calls.append(("m0a", [piece(0, e[:n // 2], "qb", "hc0", "lc0", 0, B, "h0"),
                          piece(2, e[n // 2:], "qb", "hc0", "lc0", B, 2 * B, "h0")]))
    calls.append(("m0b", [piece(0, e[:n // 4], "qb", "hc0", "lc0", 2 * B, 3 * B, "h1"),
                          piece(2, e[n // 4:n // 2], "qb", "hc0", "lc0", 3 * B, 4 * B, "h1"),
                          piece(1, e[n // 2:], "sb", "hs0", "lp0", 0, 4 * B, "h0")]))
    for t in (1, 2):
        q, p, hs = "hq%d" % (t - 1), "hp%d" % (t - 1), "h%d" % (t + 1)
        calls.append(("m%d" % t, [piece(1, e[:n // 2], q, "hc%d" % t, "lc%d" % t, 0, C // 2, hs),
                                  piece(2, e[n // 2:], q, "hc%d" % t, "lc%d" % t, C // 2, C, hs)]))
        calls.append(("m%d" % t, [piece(3, e, p, "hs%d" % t, "lp%d" % t, 0, C, hs)]))
        calls.append(("k%d" % t, [piece(0, e, "ro%d" % t, "rh%d" % t, "ri%d" % t, 0, K, hs)]))
    return calls


def _view(T, v):
    a = T[v[0]][:, v[1]:v[2]]
    return a.bitcast(dt.uint8) if SCRATCH[v[0]][2] == CODE else a


def arrivals(T, topo, rank):
    prev, me = (rank - 1) % len(T.cores), T.cores[rank]
    n = {}
    for msg, pieces in routes(T, topo, prev):
        for p in pieces:
            n[msg[:2]] = n.get(msg[:2], 0) + (len(p[1]) if p[0] is None else len(topo.engines(p[0], me)))
    return n


def carrier_program(g, core, T, topo):
    for rank in range(len(T.cores)):
        dst = T.cores[(rank + 1) % len(T.cores)]
        total = 0
        for msg, pieces in routes(T, topo, rank):
            for p in pieces:
                if p[0] != core:
                    continue
                rid, pid = topo.addr(dst, core)
                g.wait_ge(T.sem[p[5]], len(p[1]))
                g.remote_dma(_view(T, p[4]), _view(T, p[3]), T.sem[msg[:2]], T.sem.left, pid, rid, topo.mask(core, dst))
                total += len(topo.engines(core, dst))
        if total:
            g.wait_ge(T.sem.left, total)


def rank_program(g, core, T, topo):
    rank = T.rank_of(core)
    if rank is None:
        carrier_program(g, core, T, topo)
        return
    A, F = AluOpType, ActivationFunctionType
    Q = {"ve": g.vector, "ac": g.scalar, "pe": g.tensor, "po": g, "sp": g.sync}
    count = {}
    seen = {q: {} for q in Q}
    wrote, read = {}, {}

    def wait(q, tok):
        if seen[q].get(tok[0], 0) < tok[1]:
            Q[q].wait_ge(T.sem[tok[0]], tok[1])
            seen[q][tok[0]] = tok[1]

    def order(q, r, w):
        need = {}
        for k in r:
            toks = [wrote[k]] if k in wrote else []
            if k.startswith("bank"):
                toks += [t for (p, t) in read.get(k, []) if p != q]
            for t in toks:
                need[t[0]] = max(need.get(t[0], 0), t[1])
        for k in w:
            for t in ([wrote[k]] if k in wrote else []) + [t for (p, t) in read.get(k, [])]:
                need[t[0]] = max(need.get(t[0], 0), t[1])
        for s in need:
            wait(q, (s, need[s]))

    def note(q, r, w, tok):
        for k in r:
            read.setdefault(k, []).append((q, tok))
        for k in w:
            wrote[k] = tok
            read[k] = []

    def op(q, r, w, call):
        order(q, r, w)
        count[q] = count.get(q, 0) + 1
        call().then_inc(T.sem[q], 1)
        note(q, r, w, (q, count[q]))

    def dma(q, sem, total, out, in_, r, w):
        order(q, r, w)
        count[sem] = count.get(sem, 0) + 16
        Q[q].dma_start(out, in_).then_inc(T.sem[sem], 16)
        note(q, r, w, (sem, 16 * total))

    V, S = g.vector, g.scalar

    def copy(out, in_, r, w):
        op("ve", r, w, lambda: V.tensor_copy(out, in_))

    def tt(out, a, b, o, r, w):
        op("ve", r, w, lambda: V.tensor_tensor(out, a, b, o))

    def ts(out, a, s1, o1, r, w, s2=None, o2=None):
        if o2 is None:
            op("ve", r, w, lambda: V.tensor_scalar(out, a, s1, None, o1))
        else:
            op("ve", r, w, lambda: V.tensor_scalar(out, a, s1, s2, o1, o2))

    def scan(out, a, b, init, o1, o2, r, w):
        op("ve", r, w, lambda: V.tensor_tensor_scan(out, a, b, init, o1, o2))

    def fill(ap, val, w):
        op("ve", [], w, lambda: V.memset(ap, val))

    def quant(c, s, in_, r, w):
        op("ve", r, w, lambda: V.quantize_mx(c, s, in_))

    def act(out, in_, f, r, w, **kw):
        op("ac", r, w, lambda: S.activation(out, in_, f, **kw))

    def bank(b, n):
        return T.ps[:, 512 * b:512 * b + n]

    def mx(b, n, wc, wsc, xc, xsc, r):
        op("pe", r, ["bank%d" % b], lambda: g.tensor.matmul_mx(bank(b, n), wc, wsc, xc, xsc, True, True))

    def table(row, rkey, st, skey):
        scan(st[:], T.kk[:], row[:], 0.0, A.min, A.max, [rkey, "kk"], [skey])

    nxt = T.cores[(rank + 1) % len(T.cores)]
    calls = routes(T, topo, rank)
    came = arrivals(T, topo, rank)
    for m in came:
        wrote[m] = (m, came[m])

    def send(msg, r, sem):
        order("po", r, [])
        for name, pieces in calls:
            if name != msg:
                continue
            count[sem] = count.get(sem, 0) + sum(len(p[1]) for p in pieces)
            ends = []
            for p in pieces:
                to = nxt if p[0] is None else p[0]
                rid, pid = topo.addr(to, core)
                ends.append((rid, pid, _view(T, p[4] if p[0] is None else p[3]), T.sem[msg[:2] if p[0] is None else p[5]]))
            if len(pieces) == 1:
                rid, pid, out, rs = ends[0]
                g.remote_dma(out, _view(T, pieces[0][2]), rs, T.sem[sem], pid, rid, _mask(pieces[0][1]))
            else:
                g.remote_dma_fused([RemoteDMATransfer(dst_ids=[DstId(rid=x[0], pnc=x[1])], dma_engine_mask=_mask(p[1]),
                                                      remote_sem=x[3], src=_view(T, p[2]), dst=x[2])
                                    for p, x in zip(pieces, ends)], local_sem=T.sem[sem])

    for i, q in enumerate(("sp", "ac", "sp", "ac")):
        k = 3 - i
        dma(q, "dxa" if i < 2 else "dxb", 2, T.xb[:, 4 * B * i:4 * B * (i + 1)], T.x[:, W4 * k:W4 * k + 4 * B], [], ["xb%d" % i])
    for i, (q, t) in enumerate((("sp", T.la), ("ac", T.da), ("sp", T.lb), ("ac", T.db))):
        dma(q, "dl", 4, T.lst[:, 16 * i:16 * i + K], t[:], [], ["lst%d" % i])
    la, da, lb, db = [T.lst[:, 16 * i:16 * i + K] for i in range(4)]
    dma("sp", "du", 1, T.ut[:], T.u[:], [], ["ut"])

    def rest(q, k):
        dma(q, "dx", 4, T.ring[:, W4 * (2 + k) + 4 * B:W4 * (3 + k)], T.x[:, W4 * k + 4 * B:W4 * (k + 1)], [], ["xr%d" % k])
    rest("ac", 0)

    fill(T.ones[:], 1.0, ["ones"])
    op("po", [], ["nbi"], lambda: g.iota(T.nbi[:], [[0, K], [1, 16]], 128, -1))
    op("po", ["ones"], ["ident"], lambda: g.affine_select(T.ident[:], T.ones[:], [[-1, 128]], A.is_equal, 0.0, 0, 1))
    op("po", [], ["ew"], lambda: g.iota(T.ew[:, 0:4 * B], [[1, 4 * B]], 0, 0, allow_small_or_imprecise_dtypes=True))
    op("po", [], ["upi"], lambda: g.iota(T.upi[:], [[16, 8]], 0, 0))
    op("po", [], ["dw"], lambda: g.iota(T.dw[:], [[-1, 8]], 0, 0, allow_small_or_imprecise_dtypes=True))
    fill(T.et[:], 0.0, ["et"])
    fill(T.kk[:], 5 * BIG, ["kk"])
    fill(T.mm[:], 1.0, ["mm"])
    fill(T.m3[:], 1.0, ["m3"])
    fill(T.acc[:, 3 * NA - 1:3 * NA], 0.0, ["accz"])
    fill(T.kk[:, 0:C:16], -5 * BIG, ["kk"])
    fill(T.mm[:, 0:C:16], 0.0, ["mm"])
    fill(T.m3[:, 0:3 * NA:3], 0.0, ["m3"])
    ts(T.nbj[:], T.nbi[:], 15, A.bitwise_and, ["nbi"], ["nbj"])
    fill(T.tau0[:, 1:C:2], 0.0, ["tau0z"])
    ts(T.nb[:], T.nbj[:], 0.0, A.not_equal, ["nbj"], ["nb"], -BIG, A.mult)
    fill(T.tau1[:, 0:C:2], 0.0, ["tau1z"])
    for b in range(4):
        act(T.et[:, 512 * b + b:512 * (b + 1):4], T.ident[:], F.Copy, ["ident", "et"], ["et%d" % b])
    for t in range(2):
        ts(T.io2[:, C * t:C * (t + 1)], T.ew[:, 0:C], float(4 * B + C * t), A.add, ["ew"], ["io%d" % t])

    quant(T.qb[:, 0:2 * B], T.sb[:, 0:2 * B], T.xb[:, 0:8 * B], ["xb0", "xb1"], ["qa"])
    send("m0a", ["qa"], "left0")
    wait("sp", ("left0", count["left0"]))
    for k in (1, 2, 3):
        rest("sp", k)
    quant(T.qb[:, 2 * B:4 * B], T.sb[:, 2 * B:4 * B], T.xb[:, 8 * B:16 * B], ["xb2", "xb3"], ["qb"])
    send("m0b", ["qb"], "left")
    dma("sp", "dwt", 2, T.wq[:].bitcast(dt.uint8), T.wc[:], [], ["wq"])
    dma("sp", "dwt", 2, T.wp[:], T.ws[:], [], ["wp"])
    dma("sp", "dv", 1, T.vt[:], T.v[:], [], ["vt"])

    def own_offsets(d, dkey):
        ts(T.t3[:], d, float(W4), A.mult, [dkey], ["t3"])
        tt(T.t4[:], T.t3[:], T.a4[:], A.add, ["t3", "a4"], ["t4"])
        for b in range(4):
            ts(T.o16[:, K * b:K * (b + 1)], T.t4[:], float(b), A.add, ["t4"], ["o%d" % b])

    def own_parts(t, keys):
        for b in range(4):
            win = T.ring[:, W4 * (2 - t):W4 * (6 - t)].indirect(T.o16[:, K * b:K * (b + 1)])
            if t == 0 and b < 2:
                ts(T.own[:, C * b:C * (b + 1)], win, 0.5, A.mult, keys + ["o%d" % b], ["own%d" % b])
            else:
                act(T.own[:, C * b:C * (b + 1)], win, F.Copy, keys + ["o%d" % b], ["own%d" % b], scale=0.5)

    def unpack(t, n, at):
        for b in range(4):
            mx(b, n, T.qe[:, 128 * b:128 * (b + 1)], T.se[:, 128 * b:128 * (b + 1)], T["lc%d" % t][:], T["lp%d" % t][:], ["qe", "m%d" % t])
            act(T.far[:, FW * b + at:FW * b + at + n], bank(b, n), F.Copy, ["bank%d" % b], ["far%d_%d" % (b, t)], scale=0.5)

    def bounds(t):
        nd, e = T["nd%d" % t], t % 2
        ts(T.dr[:], nd[:].indirect(T.c16[:]), -1.0, A.mult, ["nd%d" % t, "c16"], ["dr"], -3.0, A.add)
        tt(T.hm[:], nd[:, e:C:2], T.dr[:, e:C:2], A.min, ["nd%d" % t, "dr"], ["hm"])
        tt(T.lo[:], nd[:, e:C:2], T.dr[:, e:C:2], A.max, ["nd%d" % t, "dr"], ["lo"])
        ts(T.hi[:], T.hm[:], 3.0, A.add, ["hm"], ["hi"])

    quant(T.qe[:], T.se[:], T.et[:], ["et"] + ["et%d" % b for b in range(4)], ["qe"])
    ts(T.a4[:], la, 4.0, A.mult, ["lst0"], ["a4"])
    ts(T.t1[:], db, -float(B), A.mult, ["lst3"], ["t1"], float(3 * B), A.add)
    own_offsets(da, "lst1")
    tt(T.t2[:], T.t1[:], lb, A.add, ["t1", "lst2"], ["t2"])
    for i in range(4):
        act(T.ring[:, W4 * (5 - i):W4 * (5 - i) + 4 * B], T.xb[:, 4 * B * i:4 * B * (i + 1)], F.Copy, ["xb%d" % i], ["xc%d" % i])
    xkeys = ["xr%d" % k for k in range(4)] + ["xc%d" % k for k in range(4)]
    copy(T.fo16[:], T.t2[:], ["t2"], ["fo16"])
    copy(T.a16[:], la, ["lst0"], ["a16"])
    copy(T.f16[:], da, ["lst1"], ["f16"])
    copy(T.up16[:, 0:8], T.upi[:], ["upi"], ["up0"])
    ts(T.up16[:, 8:16], T.upi[:], 1.0, A.add, ["upi"], ["up1"])
    quant(T.qu[:], T.su[:], T.ut[:], ["ut"], ["qu"])
    copy(T.crow[:].indirect(T.a16[:]), T.ew[:, 0:C], ["ew", "a16"], ["crow"])
    for i in range(2):
        off = T.up16[:, 8 * i:8 * i + 8]
        copy(T["u%dc" % i][:].bitcast(dt.uint32), T.qu[:].bitcast(dt.uint32).indirect(off), ["qu", "up%d" % i], ["u%dc" % i])
        act(T["u%ds" % i][:], T.su[:].indirect(off), F.Copy, ["qu", "up%d" % i], ["u%ds" % i])
    tt(T.lr[:], T.crow[:], T.nb[:], A.add, ["crow", "nb"], ["lr"])
    act(T.nd0[:], T.dw[:].indirect(T.f16[:]), F.Copy, ["dw", "f16"], ["nd0"])
    table(T.lr, "lr", T.ls, "ls")
    copy(T.c16[:], T.ls[:, 15:C:16], ["ls"], ["c16"])
    bounds(0)
    own_parts(0, xkeys)
    unpack(0, 4 * B, 0)

    for t in range(R):
        last, e = t == R - 1, t % 2
        tq, tp, hq, hp = T["tq%d" % t], T["tp%d" % t], T["hq%d" % t], T["hp%d" % t]
        fz, fkey = T.fo16, "fo16"
        if t:
            at = 4 * B + B * (t - 1)
            copy(T.ew[:, at:at + C].indirect(T["ri%d" % t][:]), T.io2[:, C * (t - 1):C * t], ["k%d" % t, "io%d" % (t - 1)], ["ewn"])
            tt(T.fr[:], T.ew[:, B * t:B * (t + 4)].indirect(T.fo16[:]), T.nb[:], A.add, ["ew", "ewn", "fo16", "nb"], ["fr"])
            table(T.fr, "fr", T.fs, "fs")
            copy(T.fz16[:], T.fs[:, 15:C:16], ["fs"], ["fz16"])
            fz, fkey = T.fz16, "fz16"
        for b in range(4):
            tt(T.z[:, b:W4:4], T.far[:, FW * b:FW * b + 4 * B + C * t].indirect(fz[:]), T.own[:, C * b:C * (b + 1)], A.add,
               ["far%d_%d" % (b, s) for s in range(t + 1)] + [fkey, "own%d" % b], ["z%d" % b])
        quant(tq[:], tp[:], T.z[:], ["z%d" % b for b in range(4)], ["tq"])
        h = T.hl[:] if last else T.ring[:, W4 * (1 - t):W4 * (2 - t)]
        hat = 0 if last else W4 * (1 - t)
        hb = T.hl if last else T.ring
        hkeys = ["h%d_%d" % (b, t) for b in range(4)]
        if not last:
            mx(4, C, T.u0c[:], T.u0s[:], tq[:], tp[:], ["tq", "u0c", "u0s"])
        for b in range(4):
            mx(b, C, T.wq[:, 128 * b:128 * (b + 1)], T.wp[:, 128 * b:128 * (b + 1)], tq[:], tp[:], ["tq", "wq", "wp"])
        if not last:
            mx(5, C, T.u0c[:], T.u0s[:], tq[:], tp[:], ["tq", "u0c", "u0s"])
        mx(6, C, T.u1c[:], T.u1s[:], tq[:], tp[:], ["tq", "u1c", "u1s"])
        for b in range(4):
            out = hb[:, hat + b:hat + W4:4]
            if last and b % 2:
                ts(out, bank(b, C), 0.03125, A.mult, ["bank%d" % b], [hkeys[b]])
            else:
                act(out, bank(b, C), F.Copy, ["bank%d" % b], [hkeys[b]], scale=0.03125)

        def sign_s1():
            act(T.sg[:], T.ps[:, 512 * 6 + e:512 * 6 + C:2], F.Sign, ["bank6"], ["sg"])
        if last:
            break
        s0 = bank(4, C)
        tt(T.sr[:], s0, T.nb[:], A.add, ["bank4", "nb"], ["sr"])
        table(T.sr, "sr", T.st, "st")

        def compare(c):
            w, col = 16 * c + 16, T.st[:, 16 * c + 15:16 * c + 16]
            ts(T.cmp[:, C * c:C * c + w], T.ps[:, 2048:2048 + w], col, A.is_ge, ["bank4", "st"], ["cl%d" % c])
            ts(T.cmp[:, C * c + w:C * (c + 1)], T.ps[:, 2048 + w:2048 + C], col, A.is_gt, ["bank4", "st"], ["cr%d" % c])

        def add_up(c):
            scan(T.sc[:, C // 2 * c:C // 2 * (c + 1)], T.cmp[:, C * c:C * c + C // 2], T.cmp[:, C * c + C // 2:C * (c + 1)],
                 T.nq[:, 16 * c + 15:16 * c + 16], A.add, A.add, ["cl%d" % c, "cr%d" % c, "nq"], ["sc%d" % c])

        def signs(i):
            c = NV + i
            act(T.sgn[:, C * i:C * (i + 1)], bank(5, C), F.Sign, ["bank5", "st"], ["sgn%d" % i],
                bias=T.st[:, 16 * c + 15:16 * c + 16], scale=-1.0)

        def sign_sums(i):
            w = 16 * (NV + i) + 16
            act(T.junk[:, C * i:C * i + w], T.sgn[:, C * i:C * i + w], F.Sign, ["sgn%d" % i], ["al%d" % i],
                bias=0.5, scale=-1.0, accum_out=T.acc[:, 3 * i + 1:3 * i + 2])
            if w < C:
                act(T.junk[:, C * i + w:C * (i + 1)], T.sgn[:, C * i + w:C * (i + 1)], F.Sign, ["sgn%d" % i], ["ar%d" % i],
                    bias=-0.5, scale=-1.0, accum_out=T.acc[:, 3 * i + 2:3 * i + 3])

        signs(0)
        for i in range(NA):
            if i + 1 < NA:
                signs(i + 1)
            sign_sums(i)
        sign_s1()
        tt(T.eq[:], s0, T.st[:], A.is_equal, ["bank4", "st"], ["eq"])
        compare(0)
        scan(T.nq[:], T.mm[:], T.eq[:], 0.0, A.mult, A.subtract, ["mm", "eq"], ["nq"])
        compare(1)
        quant(hq[:], hp[:], h, hkeys, ["hq%d" % t])
        send("m%d" % (t + 1), ["hq%d" % t], "left")
        ts(T.acc[:, 0:3 * NA:3], T.nq[:, 16 * NV + 15:C:16], 2.0, A.mult, ["nq"], ["a0"], float(C), A.add)
        add_up(0)
        for c in range(2, NV):
            compare(c)
            add_up(c - 1)
        ro = T["ro%d" % (t + 1)]
        scan(T.asum[:], T.m3[:], T.acc[:], 0.0, A.mult, A.add,
             ["m3", "a0", "accz"] + ["al%d" % i for i in range(NA)] + ["ar%d" % i for i in range(NA - 1)], ["asum"])
        add_up(NV - 1)
        ts(ro[:, NV:K], T.asum[:, 2:3 * NA:3], 0.5, A.mult, ["asum"], ["roa"])
        copy(ro[:, 0:NV], T.sc[:, C // 2 - 1:NV * (C // 2):C // 2], ["sc%d" % c for c in range(NV)], ["rov"])
        send("k%d" % (t + 1), ["roa", "rov"], "left")
        tau, nd, nn = T["tau%d" % t], T["nd%d" % t], T["nd%d" % (t + 1)]
        tt(T.p1[:], T.sg[:], T.lo[:], A.max, ["sg", "lo"], ["p1"])
        tt(tau[:, e:C:2], T.p1[:], T.hi[:], A.min, ["p1", "hi"], ["tau%d" % t])
        tt(nd[:, e:C:2], nd[:, e:C:2], tau[:, e:C:2], A.subtract, ["nd%d" % t, "tau%d" % t], ["nd%d" % t])
        tt(nn[:], tau[:].indirect(T.a16[:]), nd[:], A.add, ["tau%d" % t, "tau%dz" % t, "a16", "nd%d" % t], ["nd%d" % (t + 1)])
        tt(T.lr[:], T.nb[:], nn[:], A.subtract, ["nb", "nd%d" % (t + 1)], ["lr"])
        table(T.lr, "lr", T.ls, "ls")
        own_offsets(T.ls[:, 15:C:16], "ls")
        xkeys = xkeys + hkeys
        own_parts(t + 1, xkeys)
        unpack(t + 1, C, 4 * B + C * t)
        bounds(t + 1)
        if t == 0:
            quant(T.qv[:], T.sv[:], T.vt[:], ["vt"], ["qv"])
        else:
            copy(T.olb[:, 1:C:2], tau[:, 1:C:2], ["tau1"], ["olo"])

    sign_s1()
    quant(hq[:], hp[:], h, hkeys, ["hq2"])
    mx(4, C, T.qv[:], T.sv[:], hq[:], hp[:], ["qv", "hq2"])
    dma("sp", "dout", 7, T.oc[:], hq[:].bitcast(dt.uint8), ["hq2"], [])
    for k in range(4):
        dma("sp", "dout", 7, T.osc[4 * k:4 * k + 4, :], hp[32 * k:32 * k + 4, :], ["hq2"], [])
    act(T.ysb[:], bank(4, C), F.Copy, ["bank4"], ["ysb"])
    dma("ac", "dout", 7, T.y[:], T.ysb[:], ["ysb"], [])
    tt(T.p1[:], T.sg[:], T.lo[:], A.max, ["sg", "lo"], ["p1"])
    tt(T.p2[:], T.p1[:], T.hi[:], A.min, ["p1", "hi"], ["p2"])
    tt(T.olb[:, 0:C:2], T.p2[:], T.tau0[:, 0:C:2], A.add, ["p2", "tau0"], ["ole"])
    dma("sp", "dout", 7, T.ol[:], T.olb[0:128:16, :], ["olo", "ole"], [])
    for s in count:
        wait("po", (s, count[s]))
    for m in came:
        wait("po", (m, came[m]))
